import numpy as np
import ml_dtypes


def mxq(x, axis, fmt="e4m3"):
    dtype, down = {"e4m3": (ml_dtypes.float8_e4m3fn, 7), "e5m2": (ml_dtypes.float8_e5m2, 14)}[fmt]
    v = np.moveaxis(np.asarray(x, np.float32).astype(ml_dtypes.bfloat16).astype(np.float64), axis, -1)
    blocks = v.reshape(v.shape[:-1] + (-1, 32))
    amax = np.abs(blocks).max(-1, keepdims=True)
    byte = np.maximum(np.where(amax > 0, np.frexp(amax)[1] - 1 + 127, 0) - down, 1)
    scale = np.exp2(byte - 127.0)
    codes = (blocks / scale).astype(np.float32).astype(dtype).astype(np.float64)
    return np.moveaxis((codes * scale).reshape(v.shape), -1, axis)


WIDE = False


def mx_kscale(k):
    if not WIDE:
        return np.ones(k)
    levels = np.array([10, -10, 5, -5, 0])
    if k % 512:
        return np.exp2(np.random.permutation(np.resize(levels, k // 32))).repeat(32)
    a = np.empty((k // 512, 16))
    for p in range(k // 512):
        a[p, :8] = np.random.permutation(np.resize(levels, 8))
        for g in range(8):
            far = levels[np.abs(levels - a[p, g]) >= 10]
            a[p, g + 8] = far[np.random.randint(len(far))]
    return np.exp2(a.ravel()).repeat(32)


def f64(x):
    return np.asarray(x).astype(np.float64)


def striped8(idx):
    return np.asarray(idx).reshape(8, -1, 16).transpose(0, 2, 1).reshape(128, -1).astype(np.uint16)


def unstriped8(offs):
    return offs.reshape(8, 16, -1).transpose(0, 2, 1).reshape(8, -1).astype(np.int64)


def pick8(x, idx, run):
    r = np.arange(len(x))
    return x[r[:, None], idx[r % (8 * run) // run]]


E2M1 = np.array([0.0, 0.5, 1.0, 1.5, 2.0, 3.0, 4.0, 6.0, -0.0, -0.5, -1.0, -1.5, -2.0, -3.0, -4.0, -6.0])


def pack_weight(w, fmt):
    k, n = w.shape
    w = f64(np.asarray(w, np.float32).astype(ml_dtypes.bfloat16)).reshape(k // 32, 32, n)
    amax = np.abs(w).max(1)
    if fmt == "e4m3":
        byte = np.frexp(amax)[1] - 1 + 127 - 7
    else:
        mant, ex = np.frexp(amax / 6.0)
        byte = np.where(mant > 0.5, ex, ex - 1) + 127
    byte = np.clip(np.where(amax > 0, byte, 1), 1, 254)
    scaled = (w * np.exp2(127.0 - byte)[:, None, :]).reshape(k, n).astype(np.float32)
    by_word = np.ascontiguousarray(scaled.reshape(k // 512, 128, 4, n).transpose(0, 1, 3, 2))
    if fmt == "e4m3":
        words = by_word.astype(ml_dtypes.float8_e4m3fn).view(np.uint8)
    else:
        c = by_word.astype(ml_dtypes.float4_e2m1fn).view(np.uint8) & 0xF
        words = (c[..., 0::2] | (c[..., 1::2] << 4)).reshape(k // 512, 128, 2 * n)
    return np.ascontiguousarray(words), np.ascontiguousarray(byte.astype(np.uint8).reshape(k // 512, 16, n))


def unpack_weight(words, scales, fmt):
    g, _, n = scales.shape
    words = np.ascontiguousarray(words).reshape(g, 128, n, -1)
    if fmt == "e4m3":
        vals = words.view(ml_dtypes.float8_e4m3fn).astype(np.float64)
    else:
        nib = np.empty((g, 128, n, 4), np.uint8)
        nib[..., 0::2] = words & 0xF
        nib[..., 1::2] = words >> 4
        vals = E2M1[nib]
    vals = vals * np.repeat(np.exp2(scales.astype(np.float64) - 127.0), 8, axis=1)[..., None]
    return vals.transpose(0, 1, 3, 2).reshape(g * 512, n)


D, T, U, I, J, Q = 512, 1024, 1024, 512, 256, 128


def setup_inputs():
    n = np.random.standard_normal
    idx = np.stack([np.random.permutation(T)[:I] for _ in range(8)])
    idx2 = np.stack([np.random.permutation(U)[:J] for _ in range(8)])
    idx3 = np.stack([np.random.permutation(I)[:J] for _ in range(8)])
    idx4 = np.stack([np.random.permutation(U)[:I] for _ in range(8)])
    idx5 = np.stack([np.random.permutation(U)[:I] for _ in range(8)])
    fd = mx_kscale(D)
    keysp = pack_weight(n((D, T)) / fd[:, None], "e2m1")
    notesp = pack_weight(n((D, U)) / fd[:, None], "e4m3")
    return {
        "query": (n((D, Q)) * 1.0 / np.sqrt(D) * fd[:, None]).astype(np.float32),
        "keys_words": keysp[0],
        "keys_scales": keysp[1],
        "notes_words": notesp[0],
        "notes_scales": notesp[1],
        "offs": striped8(idx),
        "offs2": striped8(idx2),
        "offs3": striped8(idx3),
        "offs4": striped8(idx4),
        "offs5": striped8(idx5),
    }


def reference(query, keys_words, keys_scales, notes_words, notes_scales, offs, offs2, offs3, offs4, offs5):
    idx = unstriped8(offs)
    idx2 = unstriped8(offs2)
    idx3 = unstriped8(offs3)
    idx4 = unstriped8(offs4)
    idx5 = unstriped8(offs5)
    keysu = unpack_weight(keys_words, keys_scales, "e2m1")
    notesu = unpack_weight(notes_words, notes_scales, "e4m3")
    queryq = mxq(f64(query), 0, "e4m3")
    a = queryq.T @ keysu
    b = queryq.T @ notesu
    w = pick8(a, idx, 16) * 1.25
    v = np.maximum(pick8(b, idx2, 16), pick8(w, idx3, 16))
    f1 = np.zeros((Q, U))
    f1[np.arange(Q)[:, None], idx2[np.arange(Q) % 128 // 16]] = v
    cc = b + f1
    y = np.maximum(pick8(cc, idx4, 16), pick8(b, idx5, 16))
    return y

@@ -1,0 +1,127 @@
+from contextlib import ExitStack
+
+import concourse.mybir as mybir
+
+D, T, U, I, J, Q = 512, 1024, 1024, 512, 256, 128
+FLOPS = 2 * D * Q * (T + U)
+
+F32 = mybir.dt.float32
+BF16 = mybir.dt.bfloat16
+I32 = mybir.dt.int32
+U32 = mybir.dt.uint32
+U16 = mybir.dt.uint16
+U8 = mybir.dt.uint8
+FP8X4 = mybir.dt.float8_e4m3fn_x4
+FP4X4 = mybir.dt.float4_e2m1fn_x4
+ALU = mybir.AluOpType
+COPY = mybir.ActivationFunctionType.Copy
+
+P = 128
+PACK = 4
+N = 256
+W_FACTOR = 1.25
+
+
+def tile_attend_halfkept_two_kernel(tc, query, keys_words, keys_scales, notes_words, notes_scales,
+                                     offs, offs2, offs3, offs4, offs5, out):
+    nc = tc.nc
+    with ExitStack() as ctx:
+        sb = ctx.enter_context(tc.tile_pool(name="sb", bufs=1))
+        ps = ctx.enter_context(tc.psum_pool(name="ps", bufs=1))
+
+        q_raw = sb.tile([P, PACK, Q], F32, name="q_raw")
+        k_words = sb.tile([P, 2 * T], U8, name="k_words", align_bytes=64)
+        k_plane = sb.tile([P, T], U8, name="k_plane", align_bytes=64)
+        n_words = sb.tile([P, U], U32, name="n_words", align_bytes=64)
+        n_plane = sb.tile([P, U], U8, name="n_plane", align_bytes=64)
+        l1 = sb.tile([P, I // 16], U16, name="l1")
+        l2 = sb.tile([P, J // 16], U16, name="l2")
+        l3 = sb.tile([P, J // 16], U16, name="l3")
+        l4 = sb.tile([P, I // 16], U16, name="l4")
+        l5 = sb.tile([P, I // 16], U16, name="l5")
+        f1 = sb.tile([P, U], F32, name="f1")
+
+        nc.vector.memset(k_plane[:].bitcast(I32), 0)
+        nc.vector.memset(n_plane[:].bitcast(I32), 0)
+        nc.vector.memset(f1[:], 0.0)
+
+        def load_plane(plane, scales):
+            for quad in range(4):
+                nc.scalar.dma_start(
+                    out=plane[32 * quad : 32 * quad + 4, :].bitcast(I32),
+                    in_=scales[0, 4 * quad : 4 * quad + 4, :].bitcast(I32),
+                )
+
+        nc.sync.dma_start(out=q_raw[:], in_=query.rearrange("(p t) q -> p t q", t=PACK))
+        load_plane(k_plane, keys_scales)
+        nc.sync.dma_start(out=k_words[:].bitcast(I32), in_=keys_words[0].bitcast(I32))
+        nc.sync.dma_start(
+            out=n_words[:].bitcast(I32), in_=notes_words[0].rearrange("p n t -> p (n t)").bitcast(I32)
+        )
+        nc.sync.dma_start(l1[:], offs)
+        load_plane(n_plane, notes_scales)
+        nc.sync.dma_start(l3[:], offs3)
+        nc.sync.dma_start(l2[:], offs2)
+        nc.sync.dma_start(l5[:], offs5)
+        nc.sync.dma_start(l4[:], offs4)
+
+        q_bf = sb.tile([P, Q, PACK], BF16, name="q_bf", align_bytes=64)
+        nc.vector.tensor_copy(
+            out=q_bf[:].rearrange("p (c i) t -> p c t i", i=4),
+            in_=q_raw[:].rearrange("p t (c i) -> p c t i", i=4),
+        )
+        q_words = sb.tile([P, Q], U32, name="q_words", align_bytes=64)
+        q_plane = sb.tile([P, Q], U8, name="q_plane", align_bytes=64)
+        nc.vector.quantize_mx(
+            out=q_words[:].bitcast(FP8X4), scales=q_plane[:], in_=q_bf[:].rearrange("p q t -> p (q t)")
+        )
+
+        a = sb.tile([P, T], F32, name="a")
+        b = sb.tile([P, U], F32, name="b")
+
+        def scores(dst, name, moving, plane):
+            for c in range(T // N):
+                cols = slice(c * N, (c + 1) * N)
+                bank = ps.tile([P, N], F32, name="%s%d" % (name, c))
+                nc.tensor.matmul_mx(
+                    out=bank[:], lhsT=q_words[:].bitcast(FP8X4), lhsT_scale=q_plane[:],
+                    rhs=moving(c), rhs_scale=plane[:, cols], start=True, stop=True,
+                )
+                if c % 2 == 0:
+                    nc.vector.tensor_copy(out=dst[:, cols], in_=bank[:])
+                else:
+                    nc.scalar.copy(out=dst[:, cols], in_=bank[:])
+
+        scores(a, "a_bank", lambda c: k_words[:, 2 * c * N : 2 * (c + 1) * N].bitcast(FP4X4), k_plane)
+
+        w = sb.tile([P, I], F32, name="w")
+        H = I // 2
+        nc.vector.tensor_scalar(
+            out=w[:, :H], in0=a[:].indirect(l1[:, : H // 16]), scalar1=W_FACTOR, scalar2=0.0,
+            op0=ALU.mult, op1=ALU.add,
+        )
+        nc.scalar.activation(out=w[:, H:], in_=a[:].indirect(l1[:, H // 16 :]), func=COPY, scale=W_FACTOR)
+
+        scores(b, "b_bank", lambda c: n_words[:, c * N : (c + 1) * N].bitcast(FP8X4), n_plane)
+
+        w3 = sb.tile([P, J], F32, name="w3")
+        b2 = sb.tile([P, J], F32, name="b2")
+        nc.vector.tensor_copy(out=w3[:], in_=w[:].indirect(l3[:]))
+        nc.scalar.activation(out=b2[:], in_=b[:].indirect(l2[:]), func=COPY)
+        v = sb.tile([P, J], F32, name="v")
+        nc.vector.tensor_tensor(out=v[:], in0=w3[:], in1=b2[:], op=ALU.max)
+        nc.vector.tensor_copy(out=f1[:].indirect(l2[:]), in_=v[:])
+
+        b5 = sb.tile([P, I], F32, name="b5")
+        nc.scalar.activation(out=b5[:], in_=b[:].indirect(l5[:]), func=COPY)
+
+        cc = sb.tile([P, U], F32, name="cc")
+        nc.vector.tensor_tensor(out=cc[:], in0=b[:], in1=f1[:], op=ALU.add)
+
+        c4 = sb.tile([P, I], F32, name="c4")
+        y = sb.tile([P, I], F32, name="y")
+        nc.scalar.activation(out=c4[:, :H], in_=cc[:].indirect(l4[:, : H // 16]), func=COPY)
+        nc.vector.tensor_copy(out=c4[:, H:], in_=cc[:].indirect(l4[:, H // 16 :]))
+        for half, queue in ((slice(0, H), nc.scalar), (slice(H, I), nc.sync)):
+            nc.vector.tensor_tensor(out=y[:, half], in0=c4[:, half], in1=b5[:, half], op=ALU.max)
+            queue.dma_start(out=out[:, half], in_=y[:, half])

@@ -45,36 +45,40 @@ def tile_attend_halfkept_two_kernel(tc, query, keys_words, keys_scales, notes_wo
         nc.vector.memset(n_plane[:].bitcast(I32), 0)
         nc.vector.memset(f1[:], 0.0)
 
-        def load_plane(plane, scales):
+        def load_plane(queue, plane, scales):
             for quad in range(4):
-                nc.scalar.dma_start(
+                queue.dma_start(
                     out=plane[32 * quad : 32 * quad + 4, :].bitcast(I32),
                     in_=scales[0, 4 * quad : 4 * quad + 4, :].bitcast(I32),
                 )
 
         nc.sync.dma_start(out=q_raw[:], in_=query.rearrange("(p t) q -> p t q", t=PACK))
-        load_plane(k_plane, keys_scales)
+        load_plane(nc.scalar, k_plane, keys_scales)
         nc.sync.dma_start(out=k_words[:].bitcast(I32), in_=keys_words[0].bitcast(I32))
         nc.sync.dma_start(
             out=n_words[:].bitcast(I32), in_=notes_words[0].rearrange("p n t -> p (n t)").bitcast(I32)
         )
+        load_plane(nc.sync, n_plane, notes_scales)
         nc.sync.dma_start(l1[:], offs)
-        load_plane(n_plane, notes_scales)
         nc.sync.dma_start(l3[:], offs3)
         nc.sync.dma_start(l2[:], offs2)
         nc.sync.dma_start(l5[:], offs5)
         nc.sync.dma_start(l4[:], offs4)
 
         q_bf = sb.tile([P, Q, PACK], BF16, name="q_bf", align_bytes=64)
-        nc.vector.tensor_copy(
-            out=q_bf[:].rearrange("p (c i) t -> p c t i", i=4),
-            in_=q_raw[:].rearrange("p t (c i) -> p c t i", i=4),
-        )
         q_words = sb.tile([P, Q], U32, name="q_words", align_bytes=64)
         q_plane = sb.tile([P, Q], U8, name="q_plane", align_bytes=64)
-        nc.vector.quantize_mx(
-            out=q_words[:].bitcast(FP8X4), scales=q_plane[:], in_=q_bf[:].rearrange("p q t -> p (q t)")
-        )
+        q_halves = (slice(0, Q // 2), slice(Q // 2, Q))
+        for rows in q_halves:
+            nc.vector.tensor_copy(
+                out=q_bf[:, rows, :].rearrange("p (c i) t -> p c t i", i=4),
+                in_=q_raw[:, :, rows].rearrange("p t (c i) -> p c t i", i=4),
+            )
+        for rows in q_halves:
+            nc.vector.quantize_mx(
+                out=q_words[:, rows].bitcast(FP8X4), scales=q_plane[:, rows],
+                in_=q_bf[:, rows, :].rearrange("p q t -> p (q t)"),
+            )
 
         a = sb.tile([P, T], F32, name="a")
         b = sb.tile([P, U], F32, name="b")

@@ -45,21 +45,22 @@ def tile_attend_halfkept_two_kernel(tc, query, keys_words, keys_scales, notes_wo
         nc.vector.memset(n_plane[:].bitcast(I32), 0)
         nc.vector.memset(f1[:], 0.0)
 
-        def load_plane(queue, plane, scales):
-            for quad in range(4):
-                queue.dma_start(
-                    out=plane[32 * quad : 32 * quad + 4, :].bitcast(I32),
-                    in_=scales[0, 4 * quad : 4 * quad + 4, :].bitcast(I32),
-                )
+        def load_quadrant(queue, plane, scales, quad):
+            queue.dma_start(
+                out=plane[32 * quad : 32 * quad + 4, :].bitcast(I32),
+                in_=scales[0, 4 * quad : 4 * quad + 4, :].bitcast(I32),
+            )
 
         nc.sync.dma_start(out=q_raw[:], in_=query.rearrange("(p t) q -> p t q", t=PACK))
-        load_plane(nc.scalar, k_plane, keys_scales)
+        for quad in range(4):
+            load_quadrant(nc.sync if quad < 2 else nc.scalar, k_plane, keys_scales, quad)
         nc.sync.dma_start(out=k_words[:].bitcast(I32), in_=keys_words[0].bitcast(I32))
         nc.sync.dma_start(
             out=n_words[:].bitcast(I32), in_=notes_words[0].rearrange("p n t -> p (n t)").bitcast(I32)
         )
-        load_plane(nc.sync, n_plane, notes_scales)
         nc.sync.dma_start(l1[:], offs)
+        for quad in range(4):
+            load_quadrant(nc.sync, n_plane, notes_scales, quad)
         nc.sync.dma_start(l3[:], offs3)
         nc.sync.dma_start(l2[:], offs2)
         nc.sync.dma_start(l5[:], offs5)

@@ -41,8 +41,6 @@ def tile_attend_halfkept_two_kernel(tc, query, keys_words, keys_scales, notes_wo
         l5 = sb.tile([P, I // 16], U16, name="l5")
         f1 = sb.tile([P, U], F32, name="f1")
 
-        nc.vector.memset(k_plane[:].bitcast(I32), 0)
-        nc.vector.memset(n_plane[:].bitcast(I32), 0)
         nc.vector.memset(f1[:], 0.0)
 
         def load_quadrant(queue, plane, scales, quad):

@@ -20,6 +20,7 @@ P = 128
 PACK = 4
 N = 256
 W_FACTOR = 1.25
+ADD_V = 768
 
 
 def tile_attend_halfkept_two_kernel(tc, query, keys_words, keys_scales, notes_words, notes_scales,
@@ -83,6 +84,7 @@ def tile_attend_halfkept_two_kernel(tc, query, keys_words, keys_scales, notes_wo
         b = sb.tile([P, U], F32, name="b")
 
         def scores(dst, name, moving, plane):
+            banks = []
             for c in range(T // N):
                 cols = slice(c * N, (c + 1) * N)
                 bank = ps.tile([P, N], F32, name="%s%d" % (name, c))
@@ -90,10 +92,12 @@ def tile_attend_halfkept_two_kernel(tc, query, keys_words, keys_scales, notes_wo
                     out=bank[:], lhsT=q_words[:].bitcast(FP8X4), lhsT_scale=q_plane[:],
                     rhs=moving(c), rhs_scale=plane[:, cols], start=True, stop=True,
                 )
+                banks.append(bank)
                 if c % 2 == 0:
                     nc.vector.tensor_copy(out=dst[:, cols], in_=bank[:])
                 else:
                     nc.scalar.copy(out=dst[:, cols], in_=bank[:])
+            return banks
 
         scores(a, "a_bank", lambda c: k_words[:, 2 * c * N : 2 * (c + 1) * N].bitcast(FP4X4), k_plane)
 
@@ -105,7 +109,7 @@ def tile_attend_halfkept_two_kernel(tc, query, keys_words, keys_scales, notes_wo
         )
         nc.scalar.activation(out=w[:, H:], in_=a[:].indirect(l1[:, H // 16 :]), func=COPY, scale=W_FACTOR)
 
-        scores(b, "b_bank", lambda c: n_words[:, c * N : (c + 1) * N].bitcast(FP8X4), n_plane)
+        b_banks = scores(b, "b_bank", lambda c: n_words[:, c * N : (c + 1) * N].bitcast(FP8X4), n_plane)
 
         w3 = sb.tile([P, J], F32, name="w3")
         b2 = sb.tile([P, J], F32, name="b2")
@@ -119,7 +123,12 @@ def tile_attend_halfkept_two_kernel(tc, query, keys_words, keys_scales, notes_wo
         nc.scalar.activation(out=b5[:], in_=b[:].indirect(l5[:]), func=COPY)
 
         cc = sb.tile([P, U], F32, name="cc")
-        nc.vector.tensor_tensor(out=cc[:], in0=b[:], in1=f1[:], op=ALU.add)
+        nc.gpsimd.tensor_tensor(out=cc[:, ADD_V:], in0=b[:, ADD_V:], in1=f1[:, ADD_V:], op=ALU.add)
+        for c0 in range(0, ADD_V, N):
+            c1 = min(c0 + N, ADD_V)
+            nc.vector.tensor_tensor(
+                out=cc[:, c0:c1], in0=b_banks[c0 // N][:, : c1 - c0], in1=f1[:, c0:c1], op=ALU.add
+            )
 
         c4 = sb.tile([P, I], F32, name="c4")
         y = sb.tile([P, I], F32, name="y")

from contextlib import ExitStack

import concourse.mybir as mybir

D, T, U, I, J, Q = 512, 1024, 1024, 512, 256, 128
FLOPS = 2 * D * Q * (T + U)

F32 = mybir.dt.float32
BF16 = mybir.dt.bfloat16
I32 = mybir.dt.int32
U32 = mybir.dt.uint32
U16 = mybir.dt.uint16
U8 = mybir.dt.uint8
FP8X4 = mybir.dt.float8_e4m3fn_x4
FP4X4 = mybir.dt.float4_e2m1fn_x4
ALU = mybir.AluOpType
COPY = mybir.ActivationFunctionType.Copy

P = 128
PACK = 4
N = 256
W_FACTOR = 1.25
ADD_V = 768


def tile_attend_halfkept_two_kernel(tc, query, keys_words, keys_scales, notes_words, notes_scales,
                                     offs, offs2, offs3, offs4, offs5, out):
    nc = tc.nc
    with ExitStack() as ctx:
        sb = ctx.enter_context(tc.tile_pool(name="sb", bufs=1))
        ps = ctx.enter_context(tc.psum_pool(name="ps", bufs=1))

        q_raw = sb.tile([P, PACK, Q], F32, name="q_raw")
        k_words = sb.tile([P, 2 * T], U8, name="k_words", align_bytes=64)
        k_plane = sb.tile([P, T], U8, name="k_plane", align_bytes=64)
        n_words = sb.tile([P, U], U32, name="n_words", align_bytes=64)
        n_plane = sb.tile([P, U], U8, name="n_plane", align_bytes=64)
        l1 = sb.tile([P, I // 16], U16, name="l1")
        l2 = sb.tile([P, J // 16], U16, name="l2")
        l3 = sb.tile([P, J // 16], U16, name="l3")
        l4 = sb.tile([P, I // 16], U16, name="l4")
        l5 = sb.tile([P, I // 16], U16, name="l5")
        f1 = sb.tile([P, U], F32, name="f1")

        nc.vector.memset(f1[:], 0.0)

        def load_quadrant(queue, plane, scales, quad):
            queue.dma_start(
                out=plane[32 * quad : 32 * quad + 4, :].bitcast(I32),
                in_=scales[0, 4 * quad : 4 * quad + 4, :].bitcast(I32),
            )

        nc.sync.dma_start(out=q_raw[:], in_=query.rearrange("(p t) q -> p t q", t=PACK))
        for quad in range(4):
            load_quadrant(nc.sync if quad < 2 else nc.scalar, k_plane, keys_scales, quad)
        nc.sync.dma_start(out=k_words[:].bitcast(I32), in_=keys_words[0].bitcast(I32))
        nc.sync.dma_start(
            out=n_words[:].bitcast(I32), in_=notes_words[0].rearrange("p n t -> p (n t)").bitcast(I32)
        )
        nc.sync.dma_start(l1[:], offs)
        for quad in range(4):
            load_quadrant(nc.sync, n_plane, notes_scales, quad)
        nc.sync.dma_start(l3[:], offs3)
        nc.sync.dma_start(l2[:], offs2)
        nc.sync.dma_start(l5[:], offs5)
        nc.sync.dma_start(l4[:], offs4)

        q_bf = sb.tile([P, Q, PACK], BF16, name="q_bf", align_bytes=64)
        q_words = sb.tile([P, Q], U32, name="q_words", align_bytes=64)
        q_plane = sb.tile([P, Q], U8, name="q_plane", align_bytes=64)
        q_halves = (slice(0, Q // 2), slice(Q // 2, Q))
        for rows in q_halves:
            nc.vector.tensor_copy(
                out=q_bf[:, rows, :].rearrange("p (c i) t -> p c t i", i=4),
                in_=q_raw[:, :, rows].rearrange("p t (c i) -> p c t i", i=4),
            )
        for rows in q_halves:
            nc.vector.quantize_mx(
                out=q_words[:, rows].bitcast(FP8X4), scales=q_plane[:, rows],
                in_=q_bf[:, rows, :].rearrange("p q t -> p (q t)"),
            )

        a = sb.tile([P, T], F32, name="a")
        b = sb.tile([P, U], F32, name="b")

        def scores(dst, name, moving, plane):
            banks = []
            for c in range(T // N):
                cols = slice(c * N, (c + 1) * N)
                bank = ps.tile([P, N], F32, name="%s%d" % (name, c))
                nc.tensor.matmul_mx(
                    out=bank[:], lhsT=q_words[:].bitcast(FP8X4), lhsT_scale=q_plane[:],
                    rhs=moving(c), rhs_scale=plane[:, cols], start=True, stop=True,
                )
                banks.append(bank)
                if c % 2 == 0:
                    nc.vector.tensor_copy(out=dst[:, cols], in_=bank[:])
                else:
                    nc.scalar.copy(out=dst[:, cols], in_=bank[:])
            return banks

        scores(a, "a_bank", lambda c: k_words[:, 2 * c * N : 2 * (c + 1) * N].bitcast(FP4X4), k_plane)

        w = sb.tile([P, I], F32, name="w")
        H = I // 2
        nc.vector.tensor_scalar(
            out=w[:, :H], in0=a[:].indirect(l1[:, : H // 16]), scalar1=W_FACTOR, scalar2=0.0,
            op0=ALU.mult, op1=ALU.add,
        )
        nc.scalar.activation(out=w[:, H:], in_=a[:].indirect(l1[:, H // 16 :]), func=COPY, scale=W_FACTOR)

        b_banks = scores(b, "b_bank", lambda c: n_words[:, c * N : (c + 1) * N].bitcast(FP8X4), n_plane)

        w3 = sb.tile([P, J], F32, name="w3")
        b2 = sb.tile([P, J], F32, name="b2")
        nc.vector.tensor_copy(out=w3[:], in_=w[:].indirect(l3[:]))
        nc.scalar.activation(out=b2[:], in_=b[:].indirect(l2[:]), func=COPY)
        v = sb.tile([P, J], F32, name="v")
        nc.vector.tensor_tensor(out=v[:], in0=w3[:], in1=b2[:], op=ALU.max)
        nc.vector.tensor_copy(out=f1[:].indirect(l2[:]), in_=v[:])

        b5 = sb.tile([P, I], F32, name="b5")
        nc.scalar.activation(out=b5[:], in_=b[:].indirect(l5[:]), func=COPY)

        cc = sb.tile([P, U], F32, name="cc")
        nc.gpsimd.tensor_tensor(out=cc[:, ADD_V:], in0=b[:, ADD_V:], in1=f1[:, ADD_V:], op=ALU.add)
        for c0 in range(0, ADD_V, N):
            c1 = min(c0 + N, ADD_V)
            nc.vector.tensor_tensor(
                out=cc[:, c0:c1], in0=b_banks[c0 // N][:, : c1 - c0], in1=f1[:, c0:c1], op=ALU.add
            )

        c4 = sb.tile([P, I], F32, name="c4")
        y = sb.tile([P, I], F32, name="y")
        nc.scalar.activation(out=c4[:, :H], in_=cc[:].indirect(l4[:, : H // 16]), func=COPY)
        nc.vector.tensor_copy(out=c4[:, H:], in_=cc[:].indirect(l4[:, H // 16 :]))
        for half, queue in ((slice(0, H), nc.scalar), (slice(H, I), nc.sync)):
            nc.vector.tensor_tensor(out=y[:, half], in0=c4[:, half], in1=b5[:, half], op=ALU.max)
            queue.dma_start(out=out[:, half], in_=y[:, half])
